import numpy as np
import ml_dtypes


def mxq(x, axis, fmt="e4m3"):
    dtype, down = {"e4m3": (ml_dtypes.float8_e4m3fn, 7), "e5m2": (ml_dtypes.float8_e5m2, 14)}[fmt]
    v = np.moveaxis(np.asarray(x, np.float32).astype(ml_dtypes.bfloat16).astype(np.float64), axis, -1)
    blocks = v.reshape(v.shape[:-1] + (-1, 32))
    amax = np.abs(blocks).max(-1, keepdims=True)
    byte = np.maximum(np.where(amax > 0, np.frexp(amax)[1] - 1 + 127, 0) - down, 1)
    scale = np.exp2(byte - 127.0)
    codes = (blocks / scale).astype(np.float32).astype(dtype).astype(np.float64)
    return np.moveaxis((codes * scale).reshape(v.shape), -1, axis)


WIDE = False


def mx_kscale(k):
    if not WIDE:
        return np.ones(k)
    levels = np.array([10, -10, 5, -5, 0])
    if k % 512:
        return np.exp2(np.random.permutation(np.resize(levels, k // 32))).repeat(32)
    a = np.empty((k // 512, 16))
    for p in range(k // 512):
        a[p, :8] = np.random.permutation(np.resize(levels, 8))
        for g in range(8):
            far = levels[np.abs(levels - a[p, g]) >= 10]
            a[p, g + 8] = far[np.random.randint(len(far))]
    return np.exp2(a.ravel()).repeat(32)


BF16 = ml_dtypes.bfloat16


def bf(x):
    return np.asarray(x, np.float32).astype(BF16)


def f64(x):
    return np.asarray(x).astype(np.float64)


B, F, D, A, O = 512, 8, 512, 128, 256


def pair_products(v):
    blocks = []
    for i in range(F - 1):
        blocks.append(v[:, i:i + 1, :] * v[:, i + 1:, :])
    return np.concatenate(blocks, axis=1)


def draw0():
    s, t = mx_kscale(D), mx_kscale(D)
    return {
        "v": bf(np.random.standard_normal((B, F, D))),
        "ga": bf((1.0 + 0.1 * np.random.standard_normal(D)) * s),
        "wa": bf(np.random.standard_normal((D, A)) / np.sqrt(D) / s[:, None]),
        "ba": bf(0.5 * np.random.standard_normal(A)),
        "h": bf(2.0 * np.random.standard_normal(A) / np.sqrt(A)),
        "gp": bf((1.0 + 0.1 * np.random.standard_normal(D)) * t),
        "wp": bf(3.0 * np.random.standard_normal((D, O)) / np.sqrt(D) / t[:, None]),
    }


def core(v, ga, wa, ba, h, gp, wp):
    e = pair_products(f64(v))
    eg = e * f64(ga)[None, None, :]
    z = np.maximum((mxq(eg, 2, "e4m3") @ mxq(f64(wa), 0, "e4m3")) + f64(ba)[None, None, :], 0.0)
    sc = np.sum(z * f64(h)[None, None, :], axis=2)
    p = np.exp(sc - np.max(sc, axis=1, keepdims=True))
    al = p / np.sum(p, axis=1, keepdims=True)
    pool = f64(gp)[None, :] * np.sum(al[:, :, None] * e, axis=1)
    return mxq(pool, 1, "e4m3") @ mxq(f64(wp), 0, "e4m3")


def e4m3fn_bytes(y):
    return np.clip(np.asarray(y, np.float64), -448.0, 448.0).astype(np.float32).astype(ml_dtypes.float8_e4m3fn).view(np.uint8)


def e4m3fn_values(b):
    return np.asarray(b, np.uint8).view(ml_dtypes.float8_e4m3fn).astype(np.float64)


def setup_inputs():
    d = draw0()
    x0 = np.asarray(d['wp']).astype(np.float64)
    s = (np.max(np.abs(x0), axis=(1,), keepdims=True) / 448.0).astype(np.float32)
    out = {}
    for k, v in d.items():
        if k == 'wp':
            out['wp_bytes'] = e4m3fn_bytes(x0 / s.astype(np.float64))
            out['wp_scale'] = s
        else:
            out[k] = v
    return out


def reference(v, ga, wa, ba, h, gp, wp_bytes, wp_scale):
    return core(v, ga, wa, ba, h, gp, e4m3fn_values(wp_bytes) * wp_scale.astype(np.float64))

from contextlib import ExitStack

import concourse.mybir as mybir
from concourse.masks import make_identity

F32 = mybir.dt.float32
BF16 = mybir.dt.bfloat16
U32 = mybir.dt.uint32
U8 = mybir.dt.uint8
FP8 = mybir.dt.float8_e4m3fn
FP8X4 = mybir.dt.float8_e4m3fn_x4
ALU = mybir.AluOpType
ACT = mybir.ActivationFunctionType
AX = mybir.AxisListType

B, F, D, A, O = 512, 8, 512, 128, 256
PAIRS = F * (F - 1) // 2
P = 128
T = 4
CHUNKS = B // P
GROUPS = 7

FLOPS = 2 * B * PAIRS * D * A + 2 * B * D * O

VEC = [(3, 7), (2, 7), (1, 7), (0, 7), (3, 6), (2, 6), (1, 6), (0, 6), (6, 7), (5, 7), (4, 7), (5, 6), (4, 6),
       (4, 5), (3, 5), (2, 5), (1, 5), (0, 5), (3, 4), (2, 4), (1, 4), (0, 4)]
POOLP = [(2, 3), (1, 3), (0, 3), (1, 2), (0, 2), (0, 1)]
GROUP = [VEC[3 * g : 3 * g + 3] + [POOLP[g]] for g in range(6)] + [VEC[18:22]]
COL = {GROUP[g][n]: 4 * g + n for g in range(GROUPS) for n in range(4)}
SCALES = [(i, j) for i in range(F - 1) for j in range(i + 1, F)]


def tile_afmpairattentionpooling_t_kernel(tc, v, ga, wa, ba, h, gp, wp_bytes, wp_scale, out):
    nc = tc.nc
    with ExitStack() as ctx:
        const = ctx.enter_context(tc.tile_pool(name="const", bufs=1))
        vpool = ctx.enter_context(tc.tile_pool(name="vpool", bufs=1))
        vtsp = ctx.enter_context(tc.tile_pool(name="vtsp", bufs=4))
        gvp = ctx.enter_context(tc.tile_pool(name="gvp", bufs=2))
        egp = ctx.enter_context(tc.tile_pool(name="egp", bufs=4))
        qp = ctx.enter_context(tc.tile_pool(name="qp", bufs=3))
        zp = ctx.enter_context(tc.tile_pool(name="zp", bufs=4))
        sp = ctx.enter_context(tc.tile_pool(name="sp", bufs=14))
        pp = ctx.enter_context(tc.tile_pool(name="pp", bufs=2))
        small = ctx.enter_context(tc.tile_pool(name="small", bufs=2))
        ps_vt = ctx.enter_context(tc.psum_pool(name="ps_vt", bufs=1))
        ps_z = ctx.enter_context(tc.psum_pool(name="ps_z", bufs=2))
        ps_w = ctx.enter_context(tc.psum_pool(name="ps_w", bufs=2))
        ps_sc = ctx.enter_context(tc.psum_pool(name="ps_sc", bufs=1))
        ctx.enter_context(tc.manual_schedule())

        v_sb = []
        for c in range(CHUNKS):
            v_c = vpool.tile([P, F, D], BF16, name=f"v{c}", tag=f"v{c}")
            v_sb.append(v_c)
        for f0 in (2, 0, 6, 4):
            nc.sync.dma_start(out=v_sb[0][:, f0 : f0 + 2, :], in_=v[0:P, f0 : f0 + 2, :])
        ga_b = const.tile([P, T], BF16, name="ga_b")
        nc.scalar.dma_start(out=ga_b[:], in_=ga.rearrange("(p t) -> p t", t=T))
        ba_b = const.tile([P, 1], BF16, name="ba_b")
        nc.scalar.dma_start(out=ba_b[:], in_=ba.rearrange("(a o) -> a o", o=1))
        h_b = const.tile([P, 1], BF16, name="h_b")
        nc.scalar.dma_start(out=h_b[:], in_=h.rearrange("(a o) -> a o", o=1))
        wa_sb = const.tile([P, T, A], BF16, name="wa_sb")
        nc.sync.dma_start(out=wa_sb[:], in_=wa.rearrange("(p t) a -> p t a", t=T))
        nc.sync.dma_start(out=v_sb[1][:], in_=v[P : 2 * P])
        wp8 = const.tile([P, T, O], U8, name="wp8")
        nc.sync.dma_start(out=wp8[:], in_=wp_bytes.rearrange("(p t) n -> p t n", t=T))
        wps = const.tile([P, T], F32, name="wps")
        nc.sync.dma_start(out=wps[:], in_=wp_scale.rearrange("(p t) o -> p (t o)", t=T))
        for c in range(2, CHUNKS):
            nc.sync.dma_start(out=v_sb[c][:], in_=v[c * P : (c + 1) * P])
        gpb = const.tile([P, D], BF16, name="gpb")
        nc.sync.dma_start(out=gpb[:], in_=gp.partition_broadcast(P))

        warm = const.tile([P, 1], F32, name="warm")
        nc.vector.memset(warm[:], 0.0)
        nc.scalar.activation(out=warm[:], in_=warm[:], func=ACT.Exp)
        ident_f = const.tile([P, P], F32, name="ident_f")
        make_identity(nc, ident_f[:])
        ident_b = const.tile([P, P], BF16, name="ident_b")
        nc.gpsimd.tensor_copy(out=ident_b[:], in_=ident_f[:])
        ga_f = const.tile([P, T], F32, name="ga_f")
        nc.vector.tensor_copy(out=ga_f[:], in_=ga_b[:])
        ba_f = const.tile([P, 1], F32, name="ba_f")
        nc.vector.tensor_copy(out=ba_f[:], in_=ba_b[:])
        h_f = const.tile([P, 1], F32, name="h_f")
        nc.vector.tensor_copy(out=h_f[:], in_=h_b[:])

        wa_g = const.tile([P, A, T], BF16, name="wa_g", align_bytes=64)
        wa_q = const.tile([P, A], U32, name="wa_q", align_bytes=64)
        wa_s = const.tile([P, A], U8, name="wa_s", align_bytes=64)
        wp_g = const.tile([P, O, T], BF16, name="wp_g", align_bytes=64)
        wp_q = const.tile([P, O], U32, name="wp_q", align_bytes=64)
        wp_s = const.tile([P, O], U8, name="wp_s", align_bytes=64)

        def prepare_wa():
            nc.vector.tensor_copy(out=wa_g[:], in_=wa_sb[:].rearrange("p t a -> p a t"))

        def quantize_wa():
            nc.vector.quantize_mx(out=wa_q[:].bitcast(FP8X4), scales=wa_s[:], in_=wa_g[:].rearrange("p a t -> p (a t)"))

        def prepare_wp():
            for t in range(T):
                nc.vector.tensor_scalar(out=wp_g[:, :, t], in0=wp8[:, t, :].bitcast(FP8), scalar1=wps[:, t : t + 1], scalar2=None, op0=ALU.mult)

        def quantize_wp():
            nc.vector.quantize_mx(out=wp_q[:].bitcast(FP8X4), scales=wp_s[:], in_=wp_g[:].rearrange("p n t -> p (n t)"))

        vt = {}
        vts = {}
        gv = {}
        eg = {}
        codes = {}
        zps = {}
        z = {}
        sc = {}
        pexp = {}
        rsum = {}
        s_t = {}
        w_t = {}
        p_t = {}
        pool_t = {}

        def transpose_fields(c, f0):
            if c not in vts:
                vts_c = vtsp.tile([P, F * D], BF16, name="vts_c")
                vts[c] = vts_c
            tag = {0: "vtx", 2: "vtx", 4: "vt4", 6: "vt6"}[f0]
            bank = ps_vt.tile([P, 2, 2, P], F32, name="bank", tag=tag)
            words = v_sb[c][:].rearrange("b f k -> b (f k)").bitcast(F32)
            for f in range(2):
                for u in range(2):
                    lo = (f0 + f) * (D // 2)
                    nc.tensor.transpose(bank[:, f, u, :], words[:, lo + u : lo + D // 2 : 2], ident_f[:])
            for f in range(2):
                vt[c, f0 + f] = bank[:].bitcast(BF16)[:, f, :, :].rearrange("p u (b e) -> p b u e", e=2)
            return bank

        def evacuate_fields(c, f0, bank, engine):
            words = vts[c][:, f0 * D : (f0 + 2) * D].bitcast(F32).rearrange("p (f b u) -> p f b u", f=2, u=2)
            src = bank[:].rearrange("p f u b -> p f b u")
            if engine == "s":
                nc.scalar.copy(out=words, in_=src)
            else:
                nc.vector.tensor_copy(out=words, in_=src)

        def gain(c, i, eng):
            if c not in gv:
                gv_c = gvp.tile([P, F - 1, D], F32, name="gv_c")
                gv[c] = gv_c
            eng.tensor_tensor(
                out=gv[c][:, i, :].rearrange("p (b t) -> p b t", t=T),
                in0=vts[c][:, i * D : (i + 1) * D].rearrange("p (b t) -> p b t", t=T),
                in1=ga_f[:].unsqueeze(1).to_broadcast([P, P, T]),
                op=ALU.mult,
            )

        def eg_tile(S):
            if S not in eg:
                eg_s = egp.tile([P, 4, D], BF16, name="eg_s", align_bytes=64)
                eg[S] = eg_s
            return eg[S]

        def product_vector(S, n):
            c, g = divmod(S, GROUPS)
            i, j = GROUP[g][n]
            nc.vector.tensor_tensor(
                out=eg_tile(S)[:, n, :].rearrange("p (b u e) -> p b u e", u=2, e=2),
                in0=gv[c][:, i, :].rearrange("p (b u e) -> p b u e", u=2, e=2),
                in1=vt[c, j],
                op=ALU.mult,
            )

        def product_gpsimd(S):
            c, g = divmod(S, GROUPS)
            if g == 6 or c >= CHUNKS:
                return
            i, j = GROUP[g][3]
            nc.gpsimd.tensor_tensor(out=eg_tile(S)[:, 3, :], in0=gv[c][:, i, :], in1=vts[c][:, j * D : (j + 1) * D], op=ALU.mult)

        def quantize(S):
            codes_s = qp.tile([P, 4 * P], U32, name="codes_s", align_bytes=64)
            scales_s = qp.tile([P, 4 * P], U8, name="scales_s", align_bytes=64)
            nc.vector.quantize_mx(out=codes_s[:].bitcast(FP8X4), scales=scales_s[:], in_=eg[S][:].rearrange("p n k -> p (n k)"))
            codes[S] = (codes_s, scales_s)

        def scores_mx(S):
            codes_s, scales_s = codes[S]
            zps_s = ps_z.tile([P, 4 * P], F32, name="zps_s")
            nc.tensor.matmul_mx(out=zps_s[:], lhsT=wa_q[:].bitcast(FP8X4), lhsT_scale=wa_s[:], rhs=codes_s[:].bitcast(FP8X4), rhs_scale=scales_s[:], start=True, stop=True)
            zps[S] = zps_s

        def relu(S):
            z_s = zp.tile([P, 4 * P], F32, name="z_s")
            nc.scalar.activation(out=z_s[:], in_=zps[S][:], func=ACT.Relu, bias=ba_f[:, 0:1], scale=1.0)
            z[S] = z_s

        def score_sums(S):
            c, g = divmod(S, GROUPS)
            if c not in sc:
                sc_c = ps_sc.tile([P, 32], F32, name="sc_c")
                sc[c] = sc_c
            for n in range(4):
                col = 4 * g + n
                nc.tensor.matmul(sc[c][:, col : col + 1], lhsT=z[S][:, n * P : (n + 1) * P], rhs=h_f[:, 0:1], start=True, stop=True)

        def softmax_max(c):
            mx = small.tile([P, 1], F32, name="mx")
            nc.vector.reduce_max(out=mx[:], in_=sc[c][:, 0:PAIRS], axis=AX.X)
            nmx = small.tile([P, 1], F32, name="nmx")
            nc.vector.tensor_scalar(out=nmx[:], in0=mx[:], scalar1=-1.0, scalar2=None, op0=ALU.mult)
            return nmx

        def softmax_exp(c, nmx):
            pexp_c = small.tile([P, PAIRS], F32, name="pexp_c")
            sum_c = small.tile([P, 1], F32, name="sum_c")
            nc.scalar.activation(out=pexp_c[:], in_=sc[c][:, 0:PAIRS], func=ACT.Exp, bias=nmx[:, 0:1], scale=1.0, accum_out=sum_c[:, 0:1])
            pexp[c] = pexp_c
            rsum[c] = sum_c

        def softmax_sum(c):
            rs = small.tile([P, 1], F32, name="rs")
            nc.vector.reciprocal(out=rs[:], in_=rsum[c][:])
            rsum[c] = rs

        def scale_field(c, i, j, engine):
            s_c = sp.tile([P, T, P], F32, name="s_c")
            col = COL[i, j]
            src = v_sb[c][:, j, :].rearrange("b (p t) -> b t p", t=T)
            weight = pexp[c][:, col : col + 1]
            if engine == "s":
                nc.scalar.activation(out=s_c[:], in_=src, func=ACT.Copy, scale=weight)
            elif engine == "v":
                nc.vector.tensor_scalar(out=s_c[:], in0=src, scalar1=weight, scalar2=None, op0=ALU.mult)
            else:
                nc.gpsimd.tensor_scalar(out=s_c[:], in0=src, scalar1=weight, scalar2=0.0, op0=ALU.mult, op1=ALU.add)
            s_t[c, i, j] = s_c

        def sum_fields(c, i):
            w_c = ps_w.tile([P, T, P], F32, name="w_c", tag="w")
            for t in range(T):
                for j in range(i + 1, F):
                    nc.tensor.matmul(w_c[:, t, :], lhsT=s_t[c, i, j][:, t, :], rhs=ident_f[:], start=(j == i + 1), stop=(j == F - 1), is_transpose=True)
            w_t[c, i] = w_c

        def weighted_product(c, i):
            if c not in p_t:
                p_c = pp.tile([P, F - 1, T, P], F32, name="p_c")
                p_t[c] = p_c
            nc.vector.tensor_tensor(
                out=p_t[c][:, i, :, :],
                in0=w_t[c, i][:],
                in1=vts[c][:, i * D : (i + 1) * D].rearrange("p (b t) -> p t b", t=T),
                op=ALU.mult,
            )

        def sum_products(c):
            pool_c = ps_w.tile([P, T, P], F32, name="pool_c", tag="w")
            for t in range(T):
                for i in range(F - 1):
                    nc.tensor.matmul(pool_c[:, t, :], lhsT=p_t[c][:, i, t, :], rhs=ident_f[:], start=(i == 0), stop=(i == F - 2), is_transpose=True)
            pool_t[c] = pool_c

        def gain_pool(c):
            pool_b = small.tile([P, T, P], BF16, name="pool_b")
            nc.vector.scalar_tensor_tensor(out=pool_b[:], in0=pool_t[c][:], scalar=rsum[c][:, 0:1], in1=gpb[:].rearrange("b (p t) -> b t p", t=T), op0=ALU.mult, op1=ALU.mult)
            pool_t[c] = pool_b

        def transpose_pool(c):
            turned = ps_w.tile([P, T, P], BF16, name="turned", tag="w")
            for t in range(T):
                nc.tensor.transpose(turned[:, t, :], pool_t[c][:, t, :], ident_b[:])
            pool_t[c] = turned

        def interleave_pool(c):
            pg = small.tile([P, P, T], BF16, name="pg", align_bytes=64)
            nc.scalar.copy(out=pg[:], in_=pool_t[c][:].rearrange("p t b -> p b t"))
            pool_t[c] = pg

        def quantize_pool(c):
            pq = small.tile([P, P], U32, name="pq", align_bytes=64)
            psc = small.tile([P, P], U8, name="psc", align_bytes=64)
            nc.vector.quantize_mx(out=pq[:].bitcast(FP8X4), scales=psc[:], in_=pool_t[c][:].rearrange("p b t -> p (b t)"))
            pool_t[c] = (pq, psc)

        def head_mx(c):
            pq, psc = pool_t[c]
            ops = ps_w.tile([P, O], F32, name="ops", tag="w")
            nc.tensor.matmul_mx(out=ops[:], lhsT=pq[:].bitcast(FP8X4), lhsT_scale=psc[:], rhs=wp_q[:].bitcast(FP8X4), rhs_scale=wp_s[:], start=True, stop=True)
            o_sb = small.tile([P, O], F32, name="o_sb")
            nc.scalar.copy(out=o_sb[:], in_=ops[:])
            nc.sync.dma_start(out=out[c * P : (c + 1) * P, :], in_=o_sb[:])

        bank = transpose_fields(0, 2)
        evacuate_fields(0, 2, bank, "s")
        bank = transpose_fields(0, 0)
        evacuate_fields(0, 0, bank, "s")
        gain(0, 3, nc.vector)
        gain(0, 2, nc.gpsimd)
        bank = transpose_fields(0, 6)
        evacuate_fields(0, 6, bank, "s")
        gain(0, 1, nc.vector)
        gain(0, 0, nc.gpsimd)
        bank = transpose_fields(0, 4)
        evacuate_fields(0, 4, bank, "s")
        product_gpsimd(0)
        prepare_wa()
        gain(0, 6, nc.vector)
        quantize_wa()

        LAST = CHUNKS * GROUPS
        first_h = 9
        scale_slot = {}
        for n in range(len(SCALES)):
            scale_slot[SCALES[n]] = n // 4
        sum_slot = {0: 2, 1: 4, 2: 5, 3: 6, 4: 7, 5: 8, 6: 8}
        tail_engines = "vsvgvsvsvgvsvsvgvsvsvgvsvsvs"

        for S in range(LAST + 25):
            c, g = divmod(S, GROUPS)
            active = S < LAST
            hs = [(hc, S - GROUPS * hc - first_h) for hc in range(CHUNKS) if 0 <= S - GROUPS * hc - first_h <= 14]
            nmx = {}
            for hc, k in hs:
                if k == 0:
                    nmx[hc] = softmax_max(hc)
            if 0 <= S - 2 < LAST:
                relu(S - 2)
            for hc, k in hs:
                if k == 0:
                    softmax_exp(hc, nmx[hc])
                    softmax_sum(hc)
            for hc, k in hs:
                for i in range(F - 1):
                    if sum_slot[i] == k:
                        sum_fields(hc, i)
            if c + 1 < CHUNKS and g in (1, 2, 5):
                f0 = {1: 2, 2: 0, 5: 6}[g]
                bank = transpose_fields(c + 1, f0)
                evacuate_fields(c + 1, f0, bank, "s")
            if active and c > 0 and g == 0:
                bank = transpose_fields(c, 4)
                evacuate_fields(c, 4, bank, "s")
            if active:
                product_gpsimd(S + 1)
                if g == 0:
                    gain(c, 5, nc.gpsimd)
                elif g == 1:
                    gain(c, 4, nc.gpsimd)
                elif c + 1 < CHUNKS:
                    gain(c + 1, {2: 3, 3: 2, 4: 1, 5: 0, 6: 6}[g], nc.gpsimd)
            count = 4 if g == 6 else 3
            if active:
                product_vector(S, 0)
            if 0 <= S - 1 < LAST:
                quantize(S - 1)
            if active:
                product_vector(S, 1)
            for hc, k in hs:
                for i in range(F - 1):
                    if sum_slot[i] + 1 == k:
                        weighted_product(hc, i)
            if active:
                for n in range(2, count):
                    product_vector(S, n)
            if S == 3:
                prepare_wp()
            if S == 4:
                quantize_wp()
            for hc, k in hs:
                for n in range(len(SCALES)):
                    i, j = SCALES[n]
                    if scale_slot[i, j] == k:
                        scale_field(hc, i, j, tail_engines[n] if hc == CHUNKS - 1 else "s")
            if 0 <= S - 2 < LAST:
                score_sums(S - 2)
            if 0 <= S - 1 < LAST:
                scores_mx(S - 1)
            for hc, k in hs:
                if k == 10:
                    sum_products(hc)
                    gain_pool(hc)
                if k == 11:
                    transpose_pool(hc)
                    interleave_pool(hc)
                if k == 12:
                    quantize_pool(hc)
                    head_mx(hc)
